import numpy as np
import ml_dtypes


def mxq(x, axis, fmt="e4m3"):
    dtype, down = {"e4m3": (ml_dtypes.float8_e4m3fn, 7), "e5m2": (ml_dtypes.float8_e5m2, 14)}[fmt]
    v = np.moveaxis(np.asarray(x, np.float32).astype(ml_dtypes.bfloat16).astype(np.float64), axis, -1)
    blocks = v.reshape(v.shape[:-1] + (-1, 32))
    amax = np.abs(blocks).max(-1, keepdims=True)
    byte = np.maximum(np.where(amax > 0, np.frexp(amax)[1] - 1 + 127, 0) - down, 1)
    scale = np.exp2(byte - 127.0)
    codes = (blocks / scale).astype(np.float32).astype(dtype).astype(np.float64)
    return np.moveaxis((codes * scale).reshape(v.shape), -1, axis)


WIDE = False


def mx_kscale(k):
    if not WIDE:
        return np.ones(k)
    levels = np.array([10, -10, 5, -5, 0])
    if k % 512:
        return np.exp2(np.random.permutation(np.resize(levels, k // 32))).repeat(32)
    a = np.empty((k // 512, 16))
    for p in range(k // 512):
        a[p, :8] = np.random.permutation(np.resize(levels, 8))
        for g in range(8):
            far = levels[np.abs(levels - a[p, g]) >= 10]
            a[p, g + 8] = far[np.random.randint(len(far))]
    return np.exp2(a.ravel()).repeat(32)


def f64(x):
    return np.asarray(x).astype(np.float64)


def striped(idx):
    return np.tile(idx.reshape(-1, 16).T, (8, 1)).astype(np.uint16)


def unstriped(offs):
    return offs[:16].T.reshape(-1).astype(np.int64)


E2M1 = np.array([0.0, 0.5, 1.0, 1.5, 2.0, 3.0, 4.0, 6.0, -0.0, -0.5, -1.0, -1.5, -2.0, -3.0, -4.0, -6.0])


def pack_weight(w, fmt):
    k, n = w.shape
    w = f64(np.asarray(w, np.float32).astype(ml_dtypes.bfloat16)).reshape(k // 32, 32, n)
    amax = np.abs(w).max(1)
    if fmt == "e4m3":
        byte = np.frexp(amax)[1] - 1 + 127 - 7
    else:
        mant, ex = np.frexp(amax / 6.0)
        byte = np.where(mant > 0.5, ex, ex - 1) + 127
    byte = np.clip(np.where(amax > 0, byte, 1), 1, 254)
    scaled = (w * np.exp2(127.0 - byte)[:, None, :]).reshape(k, n).astype(np.float32)
    by_word = np.ascontiguousarray(scaled.reshape(k // 512, 128, 4, n).transpose(0, 1, 3, 2))
    if fmt == "e4m3":
        words = by_word.astype(ml_dtypes.float8_e4m3fn).view(np.uint8)
    else:
        c = by_word.astype(ml_dtypes.float4_e2m1fn).view(np.uint8) & 0xF
        words = (c[..., 0::2] | (c[..., 1::2] << 4)).reshape(k // 512, 128, 2 * n)
    return np.ascontiguousarray(words), np.ascontiguousarray(byte.astype(np.uint8).reshape(k // 512, 16, n))


def unpack_weight(words, scales, fmt):
    g, _, n = scales.shape
    words = np.ascontiguousarray(words).reshape(g, 128, n, -1)
    if fmt == "e4m3":
        vals = words.view(ml_dtypes.float8_e4m3fn).astype(np.float64)
    else:
        nib = np.empty((g, 128, n, 4), np.uint8)
        nib[..., 0::2] = words & 0xF
        nib[..., 1::2] = words >> 4
        vals = E2M1[nib]
    vals = vals * np.repeat(np.exp2(scales.astype(np.float64) - 127.0), 8, axis=1)[..., None]
    return vals.transpose(0, 1, 3, 2).reshape(g * 512, n)


def sigmoid(v):
    return 1.0 / (1.0 + np.exp(-np.maximum(v, -700.0)))


K, T, E, C, H, N = 512, 2048, 4, 256, 512, 384


def by_expert(wq, xq):
    return np.concatenate([wq[e].T @ xq[:, e * C:(e + 1) * C] for e in range(E)], axis=1)


def setup_inputs():
    n = np.random.standard_normal
    s = mx_kscale(K)[:, None]
    u = mx_kscale(H)
    w1 = [pack_weight(m, "e2m1") for m in n((E, K, H)) / np.sqrt(K) / s[None]]
    w3 = [pack_weight(m, "e2m1") for m in n((E, K, H)) / np.sqrt(K) / s[None] * u[None, None, :]]
    w2 = [pack_weight(m, "e2m1") for m in n((E, H, N)) / np.sqrt(H) / u[None, :, None]]
    return {
        "xT": (n((K, T)) * s).astype(np.float32),
        "w1_words": np.stack([m[0] for m in w1]),
        "w1_scales": np.stack([m[1] for m in w1]),
        "w3_words": np.stack([m[0] for m in w3]),
        "w3_scales": np.stack([m[1] for m in w3]),
        "w2_words": np.stack([m[0] for m in w2]),
        "w2_scales": np.stack([m[1] for m in w2]),
        "gate": np.tile(np.random.uniform(0.2, 1.0, E * C), (K, 1)).astype(np.float32),
        "offs": striped(np.random.permutation(T)[:E * C]),
    }


def reference(xT, w1_words, w1_scales, w3_words, w3_scales, w2_words, w2_scales, gate, offs):
    idx = unstriped(offs)
    w1 = np.stack([unpack_weight(w1_words[e], w1_scales[e], "e2m1") for e in range(E)])
    w3 = np.stack([unpack_weight(w3_words[e], w3_scales[e], "e2m1") for e in range(E)])
    w2 = np.stack([unpack_weight(w2_words[e], w2_scales[e], "e2m1") for e in range(E)])
    xq = mxq(f64(gate) * f64(xT)[:, idx], 0, "e4m3")
    h = sigmoid(by_expert(w1, xq))
    h = h * by_expert(w3, xq)
    y = by_expert(w2, mxq(h, 0, "e4m3"))
    out = np.zeros((N, T))
    out[:, idx] = y
    return out

@@ -1,0 +1,206 @@
+from contextlib import ExitStack
+
+import concourse.mybir as mybir
+from concourse.masks import make_identity
+
+K, T, E, C, H, N = 512, 2048, 4, 256, 512, 384
+S = E * C
+P = 128
+BLOCKS = S // P
+NB = N // P
+FLOPS = 2 * S * (2 * K * H + H * N)
+
+F32 = mybir.dt.float32
+BF16 = mybir.dt.bfloat16
+I32 = mybir.dt.int32
+U32 = mybir.dt.uint32
+U16 = mybir.dt.uint16
+U8 = mybir.dt.uint8
+FP8X4 = mybir.dt.float8_e4m3fn_x4
+FP4X4 = mybir.dt.float4_e2m1fn_x4
+ACT = mybir.ActivationFunctionType
+MULT = mybir.AluOpType.mult
+
+
+def tile_moe_pre_glu_sigmoid_kernel(
+    tc, xT, w1_words, w1_scales, w3_words, w3_scales, w2_words, w2_scales, gate, offs, out
+):
+    nc = tc.nc
+    with ExitStack() as ctx:
+        keep = ctx.enter_context(tc.tile_pool(name="keep", bufs=1))
+        psum = ctx.enter_context(tc.psum_pool(name="psum", bufs=1))
+
+        offsets = keep.tile([P, S // 16], U16, name="offsets")
+        nc.sync.dma_start(offsets[:], offs)
+        x_rows = xT.rearrange("(p t) c -> p t c", t=4)
+        planes = [keep.tile([P, T], F32, name=f"plane{t}") for t in range(4)]
+        nc.sync.dma_start(planes[0][:], x_rows[:, 0, :])
+        gate_rows = keep.tile([P, P], F32, name="gate_rows")
+        nc.gpsimd.memset(gate_rows[:], 0.0)
+        nc.sync.dma_start(gate_rows[0:BLOCKS, :], gate[0, :].rearrange("(b s) -> b s", s=P))
+        for t in range(1, 4):
+            nc.sync.dma_start(planes[t][:], x_rows[:, t, :])
+
+        ident = keep.tile([P, P], F32, name="ident")
+        make_identity(nc, ident[:])
+        warm = keep.tile([P, 1], F32, name="warm")
+        nc.scalar.activation(warm[:], ident[:, 0:1], ACT.Sigmoid)
+
+        def load_scales(name, scales, width):
+            plane = keep.tile([P, E, width], U8, name=name, align_bytes=64)
+            flat = plane[:].rearrange("p e n -> p (e n)").bitcast(I32)
+            nc.vector.memset(flat, 0)
+            rows = scales.rearrange("e s (q r) n -> r q (e s) n", r=4)
+            for r in range(4):
+                nc.sync.dma_start(plane[r:P:32, :, :].bitcast(I32), rows[r].bitcast(I32))
+            return plane
+
+        def load_words(name, words, e0, e1):
+            width = words.shape[3]
+            tile = keep.tile([P, e1 - e0, width], U8, name=name, align_bytes=64)
+            src = words[e0:e1].rearrange("e s p n -> p (e s) n")
+            nc.sync.dma_start(tile[:].bitcast(I32), src.bitcast(I32))
+            return [tile[:, e, :] for e in range(e1 - e0)]
+
+        w1 = load_words("w1a", w1_words, 0, 2)
+        s1 = load_scales("s1", w1_scales, H)
+        w3 = load_words("w3a", w3_words, 0, 2)
+        s3 = load_scales("s3", w3_scales, H)
+        s2 = load_scales("s2", w2_scales, N)
+        w2 = load_words("w2a", w2_words, 0, 2)
+        w1 = w1 + load_words("w1b", w1_words, 2, 4)
+        w3 = w3 + load_words("w3b", w3_words, 2, 4)
+        w2 = w2 + load_words("w2b", w2_words, 2, 4)
+
+        windows = [keep.tile([P, T], F32, name=f"window{nb}") for nb in range(NB)]
+        nc.vector.memset(windows[0][:], 0.0)
+        for nb in range(1, NB):
+            nc.scalar.copy(windows[nb][:], windows[0][:])
+
+        banks = [psum.tile([P, 512], F32, name=f"bank{i}") for i in range(8)]
+
+        gate_col = keep.tile([P, BLOCKS], F32, name="gate_col")
+        nc.tensor.transpose(banks[7][:, 0:P], gate_rows[:], ident[:])
+        nc.scalar.copy(gate_col[:], banks[7][:, 0:BLOCKS])
+
+        def offsets_of(s0, s1_):
+            return offsets[:, s0 // 16 : s1_ // 16]
+
+        gathered = {}
+
+        def gather(t, s0, s1_):
+            g = keep.tile([P, s1_ - s0], F32, name=f"g{t}_{s0}")
+            nc.vector.tensor_copy(g[:], planes[t][:].indirect(offsets_of(s0, s1_)))
+            for b in range(s0 // P, s1_ // P):
+                gathered[(t, b)] = g[:, b * P - s0 : (b + 1) * P - s0]
+
+        x_pairs = [keep.tile([P, 2, 2 * P], BF16, name=f"x_pairs{b}") for b in range(BLOCKS)]
+
+        def scale_pair(b, u, bank):
+            for i in range(2):
+                nc.tensor.transpose(bank[:, i * P : (i + 1) * P], gathered[(2 * u + i, b)], ident[:])
+            nc.scalar.activation(
+                x_pairs[b][:, u, :].rearrange("s (p i) -> s p i", i=2),
+                bank[:, 0 : 2 * P].rearrange("s (i p) -> s p i", i=2),
+                ACT.Copy,
+                scale=gate_col[:, b : b + 1],
+            )
+
+        def to_codes(name, pairs, bank, codes, scales):
+            words = pairs[:].rearrange("s u w -> s (u w)").bitcast(F32)
+            for u in range(2):
+                nc.tensor.transpose(bank[:, u * P : (u + 1) * P], words[:, u * P : (u + 1) * P], ident[:])
+            grouped = keep.tile([P, 4 * P], BF16, name=name + "_grouped", align_bytes=64)
+            nc.scalar.copy(
+                grouped[:].bitcast(F32).rearrange("p (s u) -> p s u", u=2),
+                bank[:, 0 : 2 * P].rearrange("p (u s) -> p s u", u=2),
+            )
+            nc.vector.quantize_mx(out=codes.bitcast(FP8X4), scales=scales, in_=grouped[:])
+
+        gather(0, 0, S)
+        gather(1, 0, S)
+        for b in range(BLOCKS):
+            scale_pair(b, 0, banks[b])
+        gather(2, 0, S)
+        for e in range(E):
+            gather(3, e * C, (e + 1) * C)
+
+        def tiles(name, count, width, dtype):
+            return [keep.tile([P, width], dtype, name=f"{name}{i}", align_bytes=64) for i in range(count)]
+
+        x_codes, x_scales = tiles("x_codes", BLOCKS, P, U32), tiles("x_scales", BLOCKS, P, U8)
+        h_codes, h_scales = tiles("h_codes", E, C, U32), tiles("h_scales", E, C, U8)
+
+        def bank_p(b):
+            return banks[2 * (b % 4)]
+
+        def bank_q(b):
+            return banks[2 * (b % 4) + 1]
+
+        def stage_x(b):
+            scale_pair(b, 1, bank_p(b))
+            to_codes(f"x{b}", x_pairs[b], bank_q(b), x_codes[b][:], x_scales[b][:])
+
+        def stage_h(b):
+            e = b // 2
+            for bank, w, s in ((bank_p(b), w1, s1), (bank_q(b), w3, s3)):
+                nc.tensor.matmul_mx(
+                    out=bank[:],
+                    lhsT=x_codes[b][:].bitcast(FP8X4),
+                    lhsT_scale=x_scales[b][:],
+                    rhs=w[e].bitcast(FP4X4),
+                    rhs_scale=s[:, e, :],
+                    start=True,
+                    stop=True,
+                )
+            sig = keep.tile([P, 2, P, 2], F32, name=f"sig{b}")
+            nc.scalar.activation(sig[:], bank_p(b)[:].rearrange("s (p u i) -> s u p i", u=2, i=2), ACT.Sigmoid)
+            h_pairs = keep.tile([P, 2, 2 * P], BF16, name=f"h_pairs{b}")
+            nc.vector.tensor_tensor(
+                h_pairs[:].rearrange("s u (p i) -> s u p i", i=2),
+                bank_q(b)[:].rearrange("s (p u i) -> s u p i", u=2, i=2),
+                sig[:],
+                MULT,
+            )
+            return h_pairs
+
+        def stage_t(b, h_pairs):
+            cols = slice((b % 2) * P, (b % 2 + 1) * P)
+            to_codes(f"h{b}", h_pairs, bank_q(b), h_codes[b // 2][:, cols], h_scales[b // 2][:, cols])
+
+        def piece(e0, e1, nb, bank):
+            for e in range(e0, e1):
+                nc.tensor.matmul_mx(
+                    out=bank[:, (e - e0) * C : (e - e0 + 1) * C],
+                    lhsT=w2[e][:, 2 * nb * P : 2 * (nb + 1) * P].bitcast(FP4X4),
+                    lhsT_scale=s2[:, e, nb * P : (nb + 1) * P],
+                    rhs=h_codes[e][:].bitcast(FP8X4),
+                    rhs_scale=h_scales[e][:],
+                    start=True,
+                    stop=True,
+                )
+            width = (e1 - e0) * C
+            y = keep.tile([P, width], F32, name=f"y{e0}_{nb}")
+            nc.scalar.copy(y[:], bank[:, 0:width])
+            nc.vector.tensor_copy(windows[nb][:].indirect(offsets_of(e0 * C, e1 * C)), y[:])
+
+        def store(nb):
+            nc.sync.dma_start(out[nb * P : (nb + 1) * P, :], windows[nb][:])
+
+        stage_x(0)
+        stage_x(1)
+        for b in range(BLOCKS):
+            h_pairs = stage_h(b)
+            if b >= 2:
+                e, nb = divmod(b - 2, NB)
+                piece(e, e + 1, nb, bank_p(b))
+            stage_t(b, h_pairs)
+            if b + 2 < BLOCKS:
+                stage_x(b + 2)
+        piece(2, 3, 0, bank_q(7))
+        piece(3, 4, 0, bank_p(4))
+        store(0)
+        piece(2, 4, 1, bank_q(4))
+        store(1)
+        piece(2, 4, 2, bank_p(5))
+        store(2)

@@ -34,11 +34,9 @@ def tile_moe_pre_glu_sigmoid_kernel(
         nc.sync.dma_start(offsets[:], offs)
         x_rows = xT.rearrange("(p t) c -> p t c", t=4)
         planes = [keep.tile([P, T], F32, name=f"plane{t}") for t in range(4)]
-        nc.sync.dma_start(planes[0][:], x_rows[:, 0, :])
-        gate_rows = keep.tile([P, P], F32, name="gate_rows")
-        nc.gpsimd.memset(gate_rows[:], 0.0)
-        nc.sync.dma_start(gate_rows[0:BLOCKS, :], gate[0, :].rearrange("(b s) -> b s", s=P))
-        for t in range(1, 4):
+        gate_row = keep.tile([P, 2, 4], F32, name="gate_row")
+        nc.sync.dma_start(gate_row[:], gate[0, :].rearrange("(p h j) -> p h j", h=2, j=4))
+        for t in range(4):
             nc.sync.dma_start(planes[t][:], x_rows[:, t, :])
 
         ident = keep.tile([P, P], F32, name="ident")
@@ -58,78 +56,63 @@ def tile_moe_pre_glu_sigmoid_kernel(
         def load_words(name, words, e0, e1):
             width = words.shape[3]
             tile = keep.tile([P, e1 - e0, width], U8, name=name, align_bytes=64)
-            src = words[e0:e1].rearrange("e s p n -> p (e s) n")
-            nc.sync.dma_start(tile[:].bitcast(I32), src.bitcast(I32))
+            src = words.bitcast(I32)[e0:e1, 0].rearrange("e p n -> p e n")
+            nc.sync.dma_start(tile[:].bitcast(I32), src)
             return [tile[:, e, :] for e in range(e1 - e0)]
 
-        w1 = load_words("w1a", w1_words, 0, 2)
+        w1 = load_words("w1a", w1_words, 0, 1)
         s1 = load_scales("s1", w1_scales, H)
-        w3 = load_words("w3a", w3_words, 0, 2)
+        w3 = load_words("w3a", w3_words, 0, 1)
         s3 = load_scales("s3", w3_scales, H)
+        w1 = w1 + load_words("w1b", w1_words, 1, 4)
+        w3 = w3 + load_words("w3b", w3_words, 1, 4)
         s2 = load_scales("s2", w2_scales, N)
-        w2 = load_words("w2a", w2_words, 0, 2)
-        w1 = w1 + load_words("w1b", w1_words, 2, 4)
-        w3 = w3 + load_words("w3b", w3_words, 2, 4)
-        w2 = w2 + load_words("w2b", w2_words, 2, 4)
-
-        windows = [keep.tile([P, T], F32, name=f"window{nb}") for nb in range(NB)]
-        nc.vector.memset(windows[0][:], 0.0)
-        for nb in range(1, NB):
-            nc.scalar.copy(windows[nb][:], windows[0][:])
+        w2 = load_words("w2", w2_words, 0, 4)
 
         banks = [psum.tile([P, 512], F32, name=f"bank{i}") for i in range(8)]
 
-        gate_col = keep.tile([P, BLOCKS], F32, name="gate_col")
-        nc.tensor.transpose(banks[7][:, 0:P], gate_rows[:], ident[:])
-        nc.scalar.copy(gate_col[:], banks[7][:, 0:BLOCKS])
+        gates = keep.tile([P, S], F32, name="gates")
+        for half in range(2):
+            bank = banks[6 + half]
+            for j in range(4):
+                column = gate_row[:, half, j : j + 1]
+                nc.tensor.transpose(bank[:, j * P : (j + 1) * P], column.to_broadcast([P, P]), ident[:])
+            nc.scalar.copy(
+                gates[:].rearrange("k (p h j) -> k h p j", h=2, j=4)[:, half],
+                bank[:].rearrange("k (j p) -> k p j", j=4),
+            )
+
+        windows = [keep.tile([P, T], F32, name=f"window{nb}") for nb in range(NB)]
+        for nb in range(NB):
+            for c0 in range(0, T, 512):
+                nc.gpsimd.memset(windows[nb][:, c0 : c0 + 512], 0.0)
 
         def offsets_of(s0, s1_):
             return offsets[:, s0 // 16 : s1_ // 16]
 
-        gathered = {}
+        gathered = keep.tile([P, 4, S], F32, name="gathered", align_bytes=64)
 
         def gather(t, s0, s1_):
-            g = keep.tile([P, s1_ - s0], F32, name=f"g{t}_{s0}")
-            nc.vector.tensor_copy(g[:], planes[t][:].indirect(offsets_of(s0, s1_)))
-            for b in range(s0 // P, s1_ // P):
-                gathered[(t, b)] = g[:, b * P - s0 : (b + 1) * P - s0]
-
-        x_pairs = [keep.tile([P, 2, 2 * P], BF16, name=f"x_pairs{b}") for b in range(BLOCKS)]
-
-        def scale_pair(b, u, bank):
-            for i in range(2):
-                nc.tensor.transpose(bank[:, i * P : (i + 1) * P], gathered[(2 * u + i, b)], ident[:])
-            nc.scalar.activation(
-                x_pairs[b][:, u, :].rearrange("s (p i) -> s p i", i=2),
-                bank[:, 0 : 2 * P].rearrange("s (i p) -> s p i", i=2),
-                ACT.Copy,
-                scale=gate_col[:, b : b + 1],
+            nc.vector.tensor_tensor(
+                gathered[:, t, s0:s1_], planes[t][:].indirect(offsets_of(s0, s1_)), gates[:, s0:s1_], MULT
             )
 
-        def to_codes(name, pairs, bank, codes, scales):
-            words = pairs[:].rearrange("s u w -> s (u w)").bitcast(F32)
-            for u in range(2):
-                nc.tensor.transpose(bank[:, u * P : (u + 1) * P], words[:, u * P : (u + 1) * P], ident[:])
-            grouped = keep.tile([P, 4 * P], BF16, name=name + "_grouped", align_bytes=64)
-            nc.scalar.copy(
-                grouped[:].bitcast(F32).rearrange("p (s u) -> p s u", u=2),
-                bank[:, 0 : 2 * P].rearrange("p (u s) -> p s u", u=2),
+        def interleave(grouped, s0, s1_, copy):
+            copy(
+                grouped.rearrange("p (c i t) -> p c t i", i=4, t=4),
+                gathered[:, :, s0:s1_].rearrange("p t (c i) -> p c t i", i=4),
             )
-            nc.vector.quantize_mx(out=codes.bitcast(FP8X4), scales=scales, in_=grouped[:])
 
-        gather(0, 0, S)
-        gather(1, 0, S)
-        for b in range(BLOCKS):
-            scale_pair(b, 0, banks[b])
-        gather(2, 0, S)
-        for e in range(E):
-            gather(3, e * C, (e + 1) * C)
+        def quantize(codes, scales, grouped):
+            nc.vector.quantize_mx(out=codes.bitcast(FP8X4), scales=scales, in_=grouped)
 
         def tiles(name, count, width, dtype):
             return [keep.tile([P, width], dtype, name=f"{name}{i}", align_bytes=64) for i in range(count)]
 
-        x_codes, x_scales = tiles("x_codes", BLOCKS, P, U32), tiles("x_scales", BLOCKS, P, U8)
+        x_codes, x_scales = tiles("x_codes", E, C, U32), tiles("x_scales", E, C, U8)
         h_codes, h_scales = tiles("h_codes", E, C, U32), tiles("h_scales", E, C, U8)
+        x_grouped = tiles("x_grouped", E, 4 * C, BF16)
+        h_grouped = tiles("h_grouped", E, 4 * C, BF16)
 
         def bank_p(b):
             return banks[2 * (b % 4)]
@@ -137,36 +120,46 @@ def tile_moe_pre_glu_sigmoid_kernel(
         def bank_q(b):
             return banks[2 * (b % 4) + 1]
 
-        def stage_x(b):
-            scale_pair(b, 1, bank_p(b))
-            to_codes(f"x{b}", x_pairs[b], bank_q(b), x_codes[b][:], x_scales[b][:])
-
         def stage_h(b):
             e = b // 2
+            cols = slice((b % 2) * P, (b % 2 + 1) * P)
             for bank, w, s in ((bank_p(b), w1, s1), (bank_q(b), w3, s3)):
                 nc.tensor.matmul_mx(
                     out=bank[:],
-                    lhsT=x_codes[b][:].bitcast(FP8X4),
-                    lhsT_scale=x_scales[b][:],
+                    lhsT=x_codes[e][:, cols].bitcast(FP8X4),
+                    lhsT_scale=x_scales[e][:, cols],
                     rhs=w[e].bitcast(FP4X4),
                     rhs_scale=s[:, e, :],
                     start=True,
                     stop=True,
                 )
-            sig = keep.tile([P, 2, P, 2], F32, name=f"sig{b}")
-            nc.scalar.activation(sig[:], bank_p(b)[:].rearrange("s (p u i) -> s u p i", u=2, i=2), ACT.Sigmoid)
+            if b == 1:
+                sig = gathered[:, 3, 2 * C : 4 * C]
+            else:
+                sig = keep.tile([P, H], F32, name=f"sig{b}")[:]
+            sig = sig.rearrange("s (u p i) -> s u p i", u=2, i=2)
+            nc.scalar.activation(sig, bank_p(b)[:].rearrange("s (p u i) -> s u p i", u=2, i=2), ACT.Sigmoid)
             h_pairs = keep.tile([P, 2, 2 * P], BF16, name=f"h_pairs{b}")
             nc.vector.tensor_tensor(
                 h_pairs[:].rearrange("s u (p i) -> s u p i", i=2),
                 bank_q(b)[:].rearrange("s (p u i) -> s u p i", u=2, i=2),
-                sig[:],
+                sig,
                 MULT,
             )
             return h_pairs
 
         def stage_t(b, h_pairs):
-            cols = slice((b % 2) * P, (b % 2 + 1) * P)
-            to_codes(f"h{b}", h_pairs, bank_q(b), h_codes[b // 2][:, cols], h_scales[b // 2][:, cols])
+            e, bank = b // 2, bank_q(b)
+            words = h_pairs[:].rearrange("s u w -> s (u w)").bitcast(F32)
+            for u in range(2):
+                nc.tensor.transpose(bank[:, u * P : (u + 1) * P], words[:, u * P : (u + 1) * P], ident[:])
+            grouped = h_grouped[e][:, (b % 2) * 4 * P : (b % 2 + 1) * 4 * P]
+            nc.scalar.copy(
+                grouped.bitcast(F32).rearrange("p (s u) -> p s u", u=2),
+                bank[:, 0 : 2 * P].rearrange("p (u s) -> p s u", u=2),
+            )
+            if b % 2 == 1:
+                quantize(h_codes[e][:], h_scales[e][:], h_grouped[e][:])
 
         def piece(e0, e1, nb, bank):
             for e in range(e0, e1):
@@ -187,20 +180,35 @@ def tile_moe_pre_glu_sigmoid_kernel(
         def store(nb):
             nc.sync.dma_start(out[nb * P : (nb + 1) * P, :], windows[nb][:])
 
-        stage_x(0)
-        stage_x(1)
+        for t in range(3):
+            gather(t, 0, S)
+        gather(3, 0, C)
+        first = x_grouped[0]
+        for b in range(2):
+            interleave(first[:, b * 4 * P : (b + 1) * 4 * P], b * P, (b + 1) * P, nc.scalar.copy)
+        for b in range(2):
+            cols = slice(b * P, (b + 1) * P)
+            quantize(x_codes[0][:, cols], x_scales[0][:, cols], first[:, b * 4 * P : (b + 1) * 4 * P])
+        gather(3, C, 2 * C)
         for b in range(BLOCKS):
             h_pairs = stage_h(b)
             if b >= 2:
-                e, nb = divmod(b - 2, NB)
+                e, nb = divmod(b - 1, NB)
                 piece(e, e + 1, nb, bank_p(b))
             stage_t(b, h_pairs)
-            if b + 2 < BLOCKS:
-                stage_x(b + 2)
-        piece(2, 3, 0, bank_q(7))
+            if b == 1:
+                gather(3, 2 * C, 4 * C)
+                piece(0, 1, 0, bank_p(0))
+            if b % 2 == 0 and b + 2 < BLOCKS:
+                e = b // 2 + 1
+                for half in range(2):
+                    grouped = x_grouped[e][:, half * 4 * P : (half + 1) * 4 * P]
+                    interleave(grouped, e * C + half * P, e * C + (half + 1) * P, nc.scalar.copy)
+                quantize(x_codes[e][:], x_scales[e][:], x_grouped[e][:])
+        piece(2, 3, 1, bank_q(7))
         piece(3, 4, 0, bank_p(4))
         store(0)
-        piece(2, 4, 1, bank_q(4))
+        piece(3, 4, 1, bank_q(4))
         store(1)
         piece(2, 4, 2, bank_p(5))
         store(2)

@@ -34,7 +34,7 @@ def tile_moe_pre_glu_sigmoid_kernel(
         nc.sync.dma_start(offsets[:], offs)
         x_rows = xT.rearrange("(p t) c -> p t c", t=4)
         planes = [keep.tile([P, T], F32, name=f"plane{t}") for t in range(4)]
-        gate_row = keep.tile([P, 2, 4], F32, name="gate_row")
+        gate_row = keep.tile([P, 2, 4], F32, name="gate_row", tag="reused", align_bytes=64)
         nc.sync.dma_start(gate_row[:], gate[0, :].rearrange("(p h j) -> p h j", h=2, j=4))
         for t in range(4):
             nc.sync.dma_start(planes[t][:], x_rows[:, t, :])
@@ -44,30 +44,25 @@ def tile_moe_pre_glu_sigmoid_kernel(
         warm = keep.tile([P, 1], F32, name="warm")
         nc.scalar.activation(warm[:], ident[:, 0:1], ACT.Sigmoid)
 
-        def load_scales(name, scales, width):
+        def load_scales(name, scales, width, memset):
             plane = keep.tile([P, E, width], U8, name=name, align_bytes=64)
             flat = plane[:].rearrange("p e n -> p (e n)").bitcast(I32)
-            nc.vector.memset(flat, 0)
+            memset(flat, 0)
             rows = scales.rearrange("e s (q r) n -> r q (e s) n", r=4)
             for r in range(4):
                 nc.sync.dma_start(plane[r:P:32, :, :].bitcast(I32), rows[r].bitcast(I32))
             return plane
 
-        def load_words(name, words, e0, e1):
-            width = words.shape[3]
-            tile = keep.tile([P, e1 - e0, width], U8, name=name, align_bytes=64)
-            src = words.bitcast(I32)[e0:e1, 0].rearrange("e p n -> p e n")
-            nc.sync.dma_start(tile[:].bitcast(I32), src)
-            return [tile[:, e, :] for e in range(e1 - e0)]
+        def load_words(dst, words, e0, e1):
+            dst = dst.rearrange("p (e n) -> p e n", e=e1 - e0)
+            nc.sync.dma_start(dst.bitcast(I32), words.bitcast(I32)[e0:e1, 0].rearrange("e p n -> p e n"))
+            return [dst[:, e, :] for e in range(e1 - e0)]
 
-        w1 = load_words("w1a", w1_words, 0, 1)
-        s1 = load_scales("s1", w1_scales, H)
-        w3 = load_words("w3a", w3_words, 0, 1)
-        s3 = load_scales("s3", w3_scales, H)
-        w1 = w1 + load_words("w1b", w1_words, 1, 4)
-        w3 = w3 + load_words("w3b", w3_words, 1, 4)
-        s2 = load_scales("s2", w2_scales, N)
-        w2 = load_words("w2", w2_words, 0, 4)
+        first_words = keep.tile([P, 2, 2 * H], U8, name="first_words", align_bytes=64)
+        w1 = load_words(first_words[:, 0, :], w1_words, 0, 1)
+        s1 = load_scales("s1", w1_scales, H, nc.vector.memset)
+        w3 = load_words(first_words[:, 1, :], w3_words, 0, 1)
+        s3 = load_scales("s3", w3_scales, H, nc.vector.memset)
 
         banks = [psum.tile([P, 512], F32, name=f"bank{i}") for i in range(8)]
 
@@ -77,7 +72,7 @@ def tile_moe_pre_glu_sigmoid_kernel(
             for j in range(4):
                 column = gate_row[:, half, j : j + 1]
                 nc.tensor.transpose(bank[:, j * P : (j + 1) * P], column.to_broadcast([P, P]), ident[:])
-            nc.scalar.copy(
+            (nc.scalar.copy, nc.vector.tensor_copy)[half](
                 gates[:].rearrange("k (p h j) -> k h p j", h=2, j=4)[:, half],
                 bank[:].rearrange("k (j p) -> k p j", j=4),
             )
@@ -86,6 +81,12 @@ def tile_moe_pre_glu_sigmoid_kernel(
         for nb in range(NB):
             for c0 in range(0, T, 512):
                 nc.gpsimd.memset(windows[nb][:, c0 : c0 + 512], 0.0)
+
+        later_words = keep.tile([P, 12 * H + 8 * N], U8, name="later_words", tag="reused", align_bytes=64)
+        w1 = w1 + load_words(later_words[:, 0 : 6 * H], w1_words, 1, 4)
+        w3 = w3 + load_words(later_words[:, 6 * H : 12 * H], w3_words, 1, 4)
+        w2 = load_words(later_words[:, 12 * H :], w2_words, 0, 4)
+        s2 = load_scales("s2", w2_scales, N, nc.gpsimd.memset)
 
         def offsets_of(s0, s1_):
             return offsets[:, s0 // 16 : s1_ // 16]
@@ -137,20 +138,28 @@ def tile_moe_pre_glu_sigmoid_kernel(
                 sig = gathered[:, 3, 2 * C : 4 * C]
             else:
                 sig = keep.tile([P, H], F32, name=f"sig{b}")[:]
-            sig = sig.rearrange("s (u p i) -> s u p i", u=2, i=2)
-            nc.scalar.activation(sig, bank_p(b)[:].rearrange("s (p u i) -> s u p i", u=2, i=2), ACT.Sigmoid)
-            h_pairs = keep.tile([P, 2, 2 * P], BF16, name=f"h_pairs{b}")
-            nc.vector.tensor_tensor(
-                h_pairs[:].rearrange("s u (p i) -> s u p i", i=2),
-                bank_q(b)[:].rearrange("s (p u i) -> s u p i", u=2, i=2),
-                sig,
-                MULT,
+            ordered = "s (u p i) -> s u p i"
+            permuted = "s (p u i) -> s u p i"
+            nc.scalar.activation(
+                sig.rearrange(ordered, u=2, i=2), bank_p(b)[:].rearrange(permuted, u=2, i=2), ACT.Sigmoid
             )
+            h_pairs = keep.tile([P, H], BF16, name=f"h_pairs{b}")
+            if b < 2:
+                nc.vector.tensor_tensor(
+                    h_pairs[:].rearrange(ordered, u=2, i=2),
+                    bank_q(b)[:].rearrange(permuted, u=2, i=2),
+                    sig.rearrange(ordered, u=2, i=2),
+                    MULT,
+                )
+            else:
+                linear = keep.tile([P, H], F32, name=f"linear{b}")
+                nc.scalar.copy(linear[:].rearrange(ordered, u=2, i=2), bank_q(b)[:].rearrange(permuted, u=2, i=2))
+                nc.gpsimd.tensor_tensor(h_pairs[:], linear[:], sig, MULT)
             return h_pairs
 
         def stage_t(b, h_pairs):
             e, bank = b // 2, bank_q(b)
-            words = h_pairs[:].rearrange("s u w -> s (u w)").bitcast(F32)
+            words = h_pairs[:].bitcast(F32)
             for u in range(2):
                 nc.tensor.transpose(bank[:, u * P : (u + 1) * P], words[:, u * P : (u + 1) * P], ident[:])
             grouped = h_grouped[e][:, (b % 2) * 4 * P : (b % 2 + 1) * 4 * P]

@@ -41,8 +41,6 @@ def tile_moe_pre_glu_sigmoid_kernel(
 
         ident = keep.tile([P, P], F32, name="ident")
         make_identity(nc, ident[:])
-        warm = keep.tile([P, 1], F32, name="warm")
-        nc.scalar.activation(warm[:], ident[:, 0:1], ACT.Sigmoid)
 
         def load_scales(name, scales, width, memset):
             plane = keep.tile([P, E, width], U8, name=name, align_bytes=64)
@@ -72,7 +70,7 @@ def tile_moe_pre_glu_sigmoid_kernel(
             for j in range(4):
                 column = gate_row[:, half, j : j + 1]
                 nc.tensor.transpose(bank[:, j * P : (j + 1) * P], column.to_broadcast([P, P]), ident[:])
-            (nc.scalar.copy, nc.vector.tensor_copy)[half](
+            nc.vector.tensor_copy(
                 gates[:].rearrange("k (p h j) -> k h p j", h=2, j=4)[:, half],
                 bank[:].rearrange("k (j p) -> k p j", j=4),
             )
@@ -144,7 +142,7 @@ def tile_moe_pre_glu_sigmoid_kernel(
                 sig.rearrange(ordered, u=2, i=2), bank_p(b)[:].rearrange(permuted, u=2, i=2), ACT.Sigmoid
             )
             h_pairs = keep.tile([P, H], BF16, name=f"h_pairs{b}")
-            if b < 2:
+            if b not in (2, 3, 4, 5, 6, 7):
                 nc.vector.tensor_tensor(
                     h_pairs[:].rearrange(ordered, u=2, i=2),
                     bank_q(b)[:].rearrange(permuted, u=2, i=2),
@@ -194,30 +192,34 @@ def tile_moe_pre_glu_sigmoid_kernel(
         gather(3, 0, C)
         first = x_grouped[0]
         for b in range(2):
-            interleave(first[:, b * 4 * P : (b + 1) * 4 * P], b * P, (b + 1) * P, nc.scalar.copy)
+            interleave(first[:, b * 4 * P : (b + 1) * 4 * P], b * P, (b + 1) * P, nc.vector.tensor_copy)
         for b in range(2):
             cols = slice(b * P, (b + 1) * P)
             quantize(x_codes[0][:, cols], x_scales[0][:, cols], first[:, b * 4 * P : (b + 1) * 4 * P])
         gather(3, C, 2 * C)
+        interleave(x_grouped[1][:], C, 2 * C, nc.vector.tensor_copy)
+        quantize(x_codes[1][:], x_scales[1][:], x_grouped[1][:])
         for b in range(BLOCKS):
             h_pairs = stage_h(b)
-            if b >= 2:
-                e, nb = divmod(b - 1, NB)
-                piece(e, e + 1, nb, bank_p(b))
             stage_t(b, h_pairs)
             if b == 1:
                 gather(3, 2 * C, 4 * C)
-                piece(0, 1, 0, bank_p(0))
-            if b % 2 == 0 and b + 2 < BLOCKS:
-                e = b // 2 + 1
+            if b in (3, 5):
+                piece(b // 2 - 1, b // 2, 2, bank_q(b))
+            if b in (1, 3, 5):
+                piece(b // 2, b // 2 + 1, 0, bank_p(b - 1))
+            if b in (1, 3):
+                piece(b // 2, b // 2 + 1, 1, bank_p(b))
+            if b in {2: 2, 4: 3}:
+                e = {2: 2, 4: 3}[b]
                 for half in range(2):
                     grouped = x_grouped[e][:, half * 4 * P : (half + 1) * 4 * P]
                     interleave(grouped, e * C + half * P, e * C + (half + 1) * P, nc.scalar.copy)
                 quantize(x_codes[e][:], x_scales[e][:], x_grouped[e][:])
         piece(2, 3, 1, bank_q(7))
-        piece(3, 4, 0, bank_p(4))
+        piece(3, 4, 0, bank_p(6))
         store(0)
-        piece(3, 4, 1, bank_q(4))
+        piece(3, 4, 1, bank_p(7))
         store(1)
         piece(2, 4, 2, bank_p(5))
         store(2)

from contextlib import ExitStack

import concourse.mybir as mybir
from concourse.masks import make_identity

K, T, E, C, H, N = 512, 2048, 4, 256, 512, 384
S = E * C
P = 128
BLOCKS = S // P
NB = N // P
FLOPS = 2 * S * (2 * K * H + H * N)

F32 = mybir.dt.float32
BF16 = mybir.dt.bfloat16
I32 = mybir.dt.int32
U32 = mybir.dt.uint32
U16 = mybir.dt.uint16
U8 = mybir.dt.uint8
FP8X4 = mybir.dt.float8_e4m3fn_x4
FP4X4 = mybir.dt.float4_e2m1fn_x4
ACT = mybir.ActivationFunctionType
MULT = mybir.AluOpType.mult


def tile_moe_pre_glu_sigmoid_kernel(
    tc, xT, w1_words, w1_scales, w3_words, w3_scales, w2_words, w2_scales, gate, offs, out
):
    nc = tc.nc
    with ExitStack() as ctx:
        keep = ctx.enter_context(tc.tile_pool(name="keep", bufs=1))
        psum = ctx.enter_context(tc.psum_pool(name="psum", bufs=1))

        offsets = keep.tile([P, S // 16], U16, name="offsets")
        nc.sync.dma_start(offsets[:], offs)
        x_rows = xT.rearrange("(p t) c -> p t c", t=4)
        planes = [keep.tile([P, T], F32, name=f"plane{t}") for t in range(4)]
        gate_row = keep.tile([P, 2, 4], F32, name="gate_row", tag="reused", align_bytes=64)
        nc.sync.dma_start(gate_row[:], gate[0, :].rearrange("(p h j) -> p h j", h=2, j=4))
        for t in range(4):
            nc.sync.dma_start(planes[t][:], x_rows[:, t, :])

        ident = keep.tile([P, P], F32, name="ident")
        make_identity(nc, ident[:])

        def load_scales(name, scales, width, memset):
            plane = keep.tile([P, E, width], U8, name=name, align_bytes=64)
            flat = plane[:].rearrange("p e n -> p (e n)").bitcast(I32)
            memset(flat, 0)
            rows = scales.rearrange("e s (q r) n -> r q (e s) n", r=4)
            for r in range(4):
                nc.sync.dma_start(plane[r:P:32, :, :].bitcast(I32), rows[r].bitcast(I32))
            return plane

        def load_words(dst, words, e0, e1):
            dst = dst.rearrange("p (e n) -> p e n", e=e1 - e0)
            nc.sync.dma_start(dst.bitcast(I32), words.bitcast(I32)[e0:e1, 0].rearrange("e p n -> p e n"))
            return [dst[:, e, :] for e in range(e1 - e0)]

        first_words = keep.tile([P, 2, 2 * H], U8, name="first_words", align_bytes=64)
        w1 = load_words(first_words[:, 0, :], w1_words, 0, 1)
        s1 = load_scales("s1", w1_scales, H, nc.vector.memset)
        w3 = load_words(first_words[:, 1, :], w3_words, 0, 1)
        s3 = load_scales("s3", w3_scales, H, nc.vector.memset)

        banks = [psum.tile([P, 512], F32, name=f"bank{i}") for i in range(8)]

        gates = keep.tile([P, S], F32, name="gates")
        for half in range(2):
            bank = banks[6 + half]
            for j in range(4):
                column = gate_row[:, half, j : j + 1]
                nc.tensor.transpose(bank[:, j * P : (j + 1) * P], column.to_broadcast([P, P]), ident[:])
            nc.vector.tensor_copy(
                gates[:].rearrange("k (p h j) -> k h p j", h=2, j=4)[:, half],
                bank[:].rearrange("k (j p) -> k p j", j=4),
            )

        windows = [keep.tile([P, T], F32, name=f"window{nb}") for nb in range(NB)]
        for nb in range(NB):
            for c0 in range(0, T, 512):
                nc.gpsimd.memset(windows[nb][:, c0 : c0 + 512], 0.0)

        later_words = keep.tile([P, 12 * H + 8 * N], U8, name="later_words", tag="reused", align_bytes=64)
        w1 = w1 + load_words(later_words[:, 0 : 6 * H], w1_words, 1, 4)
        w3 = w3 + load_words(later_words[:, 6 * H : 12 * H], w3_words, 1, 4)
        w2 = load_words(later_words[:, 12 * H :], w2_words, 0, 4)
        s2 = load_scales("s2", w2_scales, N, nc.gpsimd.memset)

        def offsets_of(s0, s1_):
            return offsets[:, s0 // 16 : s1_ // 16]

        gathered = keep.tile([P, 4, S], F32, name="gathered", align_bytes=64)

        def gather(t, s0, s1_):
            nc.vector.tensor_tensor(
                gathered[:, t, s0:s1_], planes[t][:].indirect(offsets_of(s0, s1_)), gates[:, s0:s1_], MULT
            )

        def interleave(grouped, s0, s1_, copy):
            copy(
                grouped.rearrange("p (c i t) -> p c t i", i=4, t=4),
                gathered[:, :, s0:s1_].rearrange("p t (c i) -> p c t i", i=4),
            )

        def quantize(codes, scales, grouped):
            nc.vector.quantize_mx(out=codes.bitcast(FP8X4), scales=scales, in_=grouped)

        def tiles(name, count, width, dtype):
            return [keep.tile([P, width], dtype, name=f"{name}{i}", align_bytes=64) for i in range(count)]

        x_codes, x_scales = tiles("x_codes", E, C, U32), tiles("x_scales", E, C, U8)
        h_codes, h_scales = tiles("h_codes", E, C, U32), tiles("h_scales", E, C, U8)
        x_grouped = tiles("x_grouped", E, 4 * C, BF16)
        h_grouped = tiles("h_grouped", E, 4 * C, BF16)

        def bank_p(b):
            return banks[2 * (b % 4)]

        def bank_q(b):
            return banks[2 * (b % 4) + 1]

        def stage_h(b):
            e = b // 2
            cols = slice((b % 2) * P, (b % 2 + 1) * P)
            for bank, w, s in ((bank_p(b), w1, s1), (bank_q(b), w3, s3)):
                nc.tensor.matmul_mx(
                    out=bank[:],
                    lhsT=x_codes[e][:, cols].bitcast(FP8X4),
                    lhsT_scale=x_scales[e][:, cols],
                    rhs=w[e].bitcast(FP4X4),
                    rhs_scale=s[:, e, :],
                    start=True,
                    stop=True,
                )
            if b == 1:
                sig = gathered[:, 3, 2 * C : 4 * C]
            else:
                sig = keep.tile([P, H], F32, name=f"sig{b}")[:]
            ordered = "s (u p i) -> s u p i"
            permuted = "s (p u i) -> s u p i"
            nc.scalar.activation(
                sig.rearrange(ordered, u=2, i=2), bank_p(b)[:].rearrange(permuted, u=2, i=2), ACT.Sigmoid
            )
            h_pairs = keep.tile([P, H], BF16, name=f"h_pairs{b}")
            if b not in (2, 3, 4, 5, 6, 7):
                nc.vector.tensor_tensor(
                    h_pairs[:].rearrange(ordered, u=2, i=2),
                    bank_q(b)[:].rearrange(permuted, u=2, i=2),
                    sig.rearrange(ordered, u=2, i=2),
                    MULT,
                )
            else:
                linear = keep.tile([P, H], F32, name=f"linear{b}")
                nc.scalar.copy(linear[:].rearrange(ordered, u=2, i=2), bank_q(b)[:].rearrange(permuted, u=2, i=2))
                nc.gpsimd.tensor_tensor(h_pairs[:], linear[:], sig, MULT)
            return h_pairs

        def stage_t(b, h_pairs):
            e, bank = b // 2, bank_q(b)
            words = h_pairs[:].bitcast(F32)
            for u in range(2):
                nc.tensor.transpose(bank[:, u * P : (u + 1) * P], words[:, u * P : (u + 1) * P], ident[:])
            grouped = h_grouped[e][:, (b % 2) * 4 * P : (b % 2 + 1) * 4 * P]
            nc.scalar.copy(
                grouped.bitcast(F32).rearrange("p (s u) -> p s u", u=2),
                bank[:, 0 : 2 * P].rearrange("p (u s) -> p s u", u=2),
            )
            if b % 2 == 1:
                quantize(h_codes[e][:], h_scales[e][:], h_grouped[e][:])

        def piece(e0, e1, nb, bank):
            for e in range(e0, e1):
                nc.tensor.matmul_mx(
                    out=bank[:, (e - e0) * C : (e - e0 + 1) * C],
                    lhsT=w2[e][:, 2 * nb * P : 2 * (nb + 1) * P].bitcast(FP4X4),
                    lhsT_scale=s2[:, e, nb * P : (nb + 1) * P],
                    rhs=h_codes[e][:].bitcast(FP8X4),
                    rhs_scale=h_scales[e][:],
                    start=True,
                    stop=True,
                )
            width = (e1 - e0) * C
            y = keep.tile([P, width], F32, name=f"y{e0}_{nb}")
            nc.scalar.copy(y[:], bank[:, 0:width])
            nc.vector.tensor_copy(windows[nb][:].indirect(offsets_of(e0 * C, e1 * C)), y[:])

        def store(nb):
            nc.sync.dma_start(out[nb * P : (nb + 1) * P, :], windows[nb][:])

        for t in range(3):
            gather(t, 0, S)
        gather(3, 0, C)
        first = x_grouped[0]
        for b in range(2):
            interleave(first[:, b * 4 * P : (b + 1) * 4 * P], b * P, (b + 1) * P, nc.vector.tensor_copy)
        for b in range(2):
            cols = slice(b * P, (b + 1) * P)
            quantize(x_codes[0][:, cols], x_scales[0][:, cols], first[:, b * 4 * P : (b + 1) * 4 * P])
        gather(3, C, 2 * C)
        interleave(x_grouped[1][:], C, 2 * C, nc.vector.tensor_copy)
        quantize(x_codes[1][:], x_scales[1][:], x_grouped[1][:])
        for b in range(BLOCKS):
            h_pairs = stage_h(b)
            stage_t(b, h_pairs)
            if b == 1:
                gather(3, 2 * C, 4 * C)
            if b in (3, 5):
                piece(b // 2 - 1, b // 2, 2, bank_q(b))
            if b in (1, 3, 5):
                piece(b // 2, b // 2 + 1, 0, bank_p(b - 1))
            if b in (1, 3):
                piece(b // 2, b // 2 + 1, 1, bank_p(b))
            if b in {2: 2, 4: 3}:
                e = {2: 2, 4: 3}[b]
                for half in range(2):
                    grouped = x_grouped[e][:, half * 4 * P : (half + 1) * 4 * P]
                    interleave(grouped, e * C + half * P, e * C + (half + 1) * P, nc.scalar.copy)
                quantize(x_codes[e][:], x_scales[e][:], x_grouped[e][:])
        piece(2, 3, 1, bank_q(7))
        piece(3, 4, 0, bank_p(6))
        store(0)
        piece(3, 4, 1, bank_p(7))
        store(1)
        piece(2, 4, 2, bank_p(5))
        store(2)
